import numpy as np
import ml_dtypes


def mxq(x, axis, fmt="e4m3"):
    dtype, down = {"e4m3": (ml_dtypes.float8_e4m3fn, 7), "e5m2": (ml_dtypes.float8_e5m2, 14)}[fmt]
    v = np.moveaxis(np.asarray(x, np.float32).astype(ml_dtypes.bfloat16).astype(np.float64), axis, -1)
    blocks = v.reshape(v.shape[:-1] + (-1, 32))
    amax = np.abs(blocks).max(-1, keepdims=True)
    byte = np.maximum(np.where(amax > 0, np.frexp(amax)[1] - 1 + 127, 0) - down, 1)
    scale = np.exp2(byte - 127.0)
    codes = (blocks / scale).astype(np.float32).astype(dtype).astype(np.float64)
    return np.moveaxis((codes * scale).reshape(v.shape), -1, axis)


WIDE = False


def mx_kscale(k):
    if not WIDE:
        return np.ones(k)
    levels = np.array([10, -10, 5, -5, 0])
    if k % 512:
        return np.exp2(np.random.permutation(np.resize(levels, k // 32))).repeat(32)
    a = np.empty((k // 512, 16))
    for p in range(k // 512):
        a[p, :8] = np.random.permutation(np.resize(levels, 8))
        for g in range(8):
            far = levels[np.abs(levels - a[p, g]) >= 10]
            a[p, g + 8] = far[np.random.randint(len(far))]
    return np.exp2(a.ravel()).repeat(32)


def f64(x):
    return np.asarray(x).astype(np.float64)


def striped(idx):
    return np.tile(idx.reshape(-1, 16).T, (8, 1)).astype(np.uint16)


def unstriped(offs):
    return offs[:16].T.reshape(-1).astype(np.int64)


E2M1 = np.array([0.0, 0.5, 1.0, 1.5, 2.0, 3.0, 4.0, 6.0, -0.0, -0.5, -1.0, -1.5, -2.0, -3.0, -4.0, -6.0])


def pack_weight(w, fmt):
    k, n = w.shape
    w = f64(np.asarray(w, np.float32).astype(ml_dtypes.bfloat16)).reshape(k // 32, 32, n)
    amax = np.abs(w).max(1)
    if fmt == "e4m3":
        byte = np.frexp(amax)[1] - 1 + 127 - 7
    else:
        mant, ex = np.frexp(amax / 6.0)
        byte = np.where(mant > 0.5, ex, ex - 1) + 127
    byte = np.clip(np.where(amax > 0, byte, 1), 1, 254)
    scaled = (w * np.exp2(127.0 - byte)[:, None, :]).reshape(k, n).astype(np.float32)
    by_word = np.ascontiguousarray(scaled.reshape(k // 512, 128, 4, n).transpose(0, 1, 3, 2))
    if fmt == "e4m3":
        words = by_word.astype(ml_dtypes.float8_e4m3fn).view(np.uint8)
    else:
        c = by_word.astype(ml_dtypes.float4_e2m1fn).view(np.uint8) & 0xF
        words = (c[..., 0::2] | (c[..., 1::2] << 4)).reshape(k // 512, 128, 2 * n)
    return np.ascontiguousarray(words), np.ascontiguousarray(byte.astype(np.uint8).reshape(k // 512, 16, n))


def unpack_weight(words, scales, fmt):
    g, _, n = scales.shape
    words = np.ascontiguousarray(words).reshape(g, 128, n, -1)
    if fmt == "e4m3":
        vals = words.view(ml_dtypes.float8_e4m3fn).astype(np.float64)
    else:
        nib = np.empty((g, 128, n, 4), np.uint8)
        nib[..., 0::2] = words & 0xF
        nib[..., 1::2] = words >> 4
        vals = E2M1[nib]
    vals = vals * np.repeat(np.exp2(scales.astype(np.float64) - 127.0), 8, axis=1)[..., None]
    return vals.transpose(0, 1, 3, 2).reshape(g * 512, n)


def gelu(v):
    return 0.5 * v * (1.0 + np.tanh(np.sqrt(2.0 / np.pi) * (v + 0.044715 * v**3)))


def often(T, S):
    return np.random.permutation(T)[(T * np.random.uniform(0, 1, S) ** 4).astype(np.int64)]


def bf(x):
    return np.asarray(x, np.float32).astype(ml_dtypes.bfloat16)


def planes(Y):
    n, m = Y.shape
    b = f64(bf(Y)).reshape(n // 32, 32, m)
    amax = np.abs(b).max(1)
    byte = np.clip(np.where(amax > 0, np.frexp(amax)[1] - 1 + 127 - 7, 1), 1, 254)
    codes = (b * np.exp2(127.0 - byte)[:, None, :]).reshape(n, m).astype(np.float32).astype(ml_dtypes.float8_e4m3fn).view(np.uint8)
    words = codes.reshape(n // 512, 128, 4, m).transpose(0, 1, 3, 2)
    return np.ascontiguousarray(words), np.ascontiguousarray(byte.astype(np.uint8).reshape(n // 512, 16, m))


K, K2, T, S, P, H, N = 512, 1024, 4096, 1024, 512, 1024, 512


def setup_inputs():
    n = np.random.standard_normal
    s = mx_kscale(K)[:, None]
    s2 = mx_kscale(K2)[:, None]
    u = mx_kscale(H)[:, None]
    d = {}
    d["tab_words"], d["tab_scales"] = pack_weight(n((K, T)) * s, "e4m3")
    d["tab2_words"], d["tab2_scales"] = pack_weight(n((K2, T)) * s2, "e4m3")
    d["tab3_words"], d["tab3_scales"] = pack_weight(n((K, T)) * s, "e4m3")
    d["offs"] = striped(np.random.permutation(T)[:S])
    d["offs2"] = striped(np.random.permutation(T)[:S])
    d["offs3"] = striped(np.random.permutation(T)[:S])
    d["pos1"] = striped(np.random.permutation(S)[:P])
    d["pos2"] = striped(often(S, P))
    d["pos3"] = striped(often(S, P))
    d["w1"] = (1.2 * n((K, H)) / s / K ** 0.5).astype(np.float32)
    d["w2"] = (1.2 * n((K2, H)) / s2 / K2 ** 0.5).astype(np.float32)
    d["w3_words"], d["w3_scales"] = pack_weight(1.2 * n((K, H)) / s / K ** 0.5, "e2m1")
    d["gain"] = (np.exp(0.4 * n(H)) * u[:, 0]).astype(np.float32)
    d["w4"] = (n((H, N)) / u / H ** 0.5 * np.exp(0.8 * n(N))[None, :]).astype(np.float32)
    return d


def reference(tab_words, tab_scales, tab2_words, tab2_scales, tab3_words, tab3_scales, offs, offs2, offs3,
              pos1, pos2, pos3, w1, w2, w3_words, w3_scales, gain, w4):
    v = unpack_weight(tab_words, tab_scales, "e4m3")[:, unstriped(offs)]
    v2 = unpack_weight(tab2_words, tab2_scales, "e4m3")[:, unstriped(offs2)]
    v3 = unpack_weight(tab3_words, tab3_scales, "e4m3")[:, unstriped(offs3)]
    a = mxq(f64(w1), 0, "e4m3").T @ v
    b = mxq(f64(w2), 0, "e4m3").T @ v2
    d = unpack_weight(w3_words, w3_scales, "e2m1").T @ v3
    bill = b[:, unstriped(pos2)]
    member_bill = np.tanh(a[:, unstriped(pos1)] * bill)
    bill_amendment = np.tanh(bill * d[:, unstriped(pos3)])
    z = f64(gain)[:, None] * (member_bill - bill_amendment)
    y = mxq(f64(w4), 0, "e4m3").T @ mxq(z, 0, "e4m3")
    words, scales = planes(y)
    return y, words, scales

@@ -1,0 +1,340 @@
+from contextlib import ExitStack
+
+import concourse.mybir as mybir
+from concourse.masks import make_identity
+
+F32 = mybir.dt.float32
+BF16 = mybir.dt.bfloat16
+I32 = mybir.dt.int32
+U32 = mybir.dt.uint32
+U16 = mybir.dt.uint16
+U8 = mybir.dt.uint8
+E4M3 = mybir.dt.float8_e4m3fn_x4
+E2M1 = mybir.dt.float4_e2m1fn_x4
+MULT = mybir.AluOpType.mult
+SUB = mybir.AluOpType.subtract
+TANH = mybir.ActivationFunctionType.Tanh
+
+P = 128
+PACK = 4
+PASS = P * PACK
+T = 4096
+S = 1024
+VOTES = 512
+H = 1024
+N = 512
+BANK = 512
+HALF = VOTES // 2
+RAWB = 3
+CHUNK = 128
+CHUNKS = VOTES // CHUNK
+
+FLOPS = 2 * H * S * (512 + 1024 + 512) + 2 * H * N * VOTES
+
+
+def tile_list_roll_call_features_kernel(
+    tc, tab_words, tab_scales, tab2_words, tab2_scales, tab3_words, tab3_scales,
+    offs, offs2, offs3, pos1, pos2, pos3, w1, w2, w3_words, w3_scales, gain, w4,
+    out_0, out_1, out_2,
+):
+    nc = tc.nc
+    with ExitStack() as ctx:
+        lists = ctx.enter_context(tc.tile_pool(name="lists", bufs=1))
+        keep = ctx.enter_context(tc.tile_pool(name="keep", bufs=1))
+        ring = ctx.enter_context(tc.tile_pool(name="ring", bufs=1))
+        psum = ctx.enter_context(tc.psum_pool(name="psum", bufs=1))
+
+        banks = [psum.tile([P, BANK], F32, name="bank%d" % i) for i in range(8)]
+        used = []
+
+        def next_bank():
+            used.append(banks[len(used) % len(banks)])
+            return used[-1]
+
+        def load_list(src, name):
+            dst = lists.tile(list(src.shape), U16, name=name)
+            nc.sync.dma_start(dst[:], src)
+            return dst
+
+        def cleared_plane(width, name, engines):
+            dst = keep.tile([P, width], U8, name=name, align_bytes=64)
+            share = width // len(engines)
+            for e, engine in enumerate(engines):
+                engine.memset(dst[:, share * e : share * (e + 1)].bitcast(I32), 0)
+            return dst
+
+        def load_scale_rows(dst, src, quadrants):
+            passes = src.shape[0]
+            for q in quadrants:
+                nc.sync.dma_start(
+                    dst[32 * q : 32 * q + 4 * passes, :].bitcast(I32),
+                    src[:, 4 * q : 4 * q + 4, :].bitcast(I32),
+                )
+
+        def table_tile(name):
+            return ring.tile([P, T], I32, name=name, tag="big", bufs=3, align_bytes=64)
+
+        def load_words(dst, words, a, cols):
+            nc.sync.dma_start(dst[:, cols], words[a].rearrange("p n t -> p (n t)").bitcast(I32)[:, cols])
+
+        def gather_words(window, offsets, name, pieces):
+            dst = keep.tile([P, S], U32, name=name, align_bytes=64)
+            n = S // pieces
+            for c in range(pieces):
+                part = offsets[:, n // 16 * c : n // 16 * (c + 1)]
+                nc.vector.tensor_copy(dst[:, n * c : n * (c + 1)], window[:].bitcast(U32).indirect(part))
+            return dst
+
+        def gather_scales(window, offsets, name):
+            dst = keep.tile([P, S], U8, name=name, align_bytes=64)
+            nc.vector.tensor_copy(dst[:], window[:].indirect(offsets[:]))
+            return dst
+
+        def load_weight(w, a, g, name):
+            raw = ring.tile([P, PACK, PASS], F32, name=name, tag="raw", bufs=RAWB)
+            rows = w[PASS * a : PASS * (a + 1), PASS * g : PASS * (g + 1)]
+            nc.sync.dma_start(raw[:], rows.rearrange("(p j) c -> p j c", j=PACK))
+            return raw
+
+        def quantize_weight(raw, name, cast):
+            grouped = ring.tile([P, PACK * PASS], BF16, name=name + "_bf", tag="grouped", bufs=2, align_bytes=64)
+            cast(
+                grouped[:].rearrange("p (t m j) -> p m j t", t=PACK, j=PACK),
+                raw[:].rearrange("p j (m t) -> p m j t", t=PACK),
+            )
+            codes = keep.tile([P, PASS], U32, name=name + "_codes", align_bytes=64)
+            scales = keep.tile([P, PASS], U8, name=name + "_scales", align_bytes=64)
+            nc.vector.quantize_mx(codes[:].bitcast(E4M3), scales[:], grouped[:])
+            return codes, scales
+
+        def first_stage(stationary, moving, name, tag, bufs):
+            rows = ring.tile([P, S], F32, name=name, tag=tag, bufs=bufs)
+            for c in range(S // BANK):
+                cols = slice(BANK * c, BANK * (c + 1))
+                acc = next_bank()
+                for a, ((lhs, lhs_scale), (rhs, rhs_scale, k)) in enumerate(zip(stationary, moving)):
+                    nc.tensor.matmul_mx(
+                        acc[:], lhsT=lhs, lhsT_scale=lhs_scale,
+                        rhs=rhs[:, cols].bitcast(E4M3), rhs_scale=rhs_scale[k:P, cols],
+                        start=(a == 0), stop=(a == len(moving) - 1),
+                    )
+                nc.scalar.copy(rows[:, cols], acc[:])
+            return rows
+
+        def slot(quantized, t):
+            codes, scales = quantized
+            return codes[:, P * t : P * (t + 1)].bitcast(E4M3), scales[:, P * t : P * (t + 1)]
+
+        whole, low, high = slice(0, T), slice(0, T // 2), slice(T // 2, T)
+        w3_plane_raw = cleared_plane(H, "w3_plane_raw", [nc.gpsimd])
+        tab3_plane = cleared_plane(T, "tab3_plane", [nc.gpsimd, nc.vector])
+        tab2_plane = cleared_plane(T, "tab2_plane", [nc.vector])
+        tab1_plane = cleared_plane(T, "tab1_plane", [nc.vector])
+        identity = keep.tile([P, P], F32, name="identity")
+        make_identity(nc, identity[:])
+        w3_raw = keep.tile([P, 2 * H], U8, name="w3_raw")
+        nc.sync.dma_start(w3_raw[:].bitcast(I32), w3_words[0].bitcast(I32))
+        idx3 = load_list(offs3, "idx3")
+        idx2 = load_list(offs2, "idx2")
+        tab3_win = table_tile("tab3_win")
+        load_words(tab3_win, tab3_words, 0, low)
+        load_scale_rows(w3_plane_raw, w3_scales, range(4))
+        load_words(tab3_win, tab3_words, 0, high)
+        load_scale_rows(tab3_plane, tab3_scales, range(4))
+        w2_raw = {(0, 0): load_weight(w2, 0, 0, "w2_raw00")}
+        tab2_win = [table_tile("tab2_win%d" % a) for a in range(2)]
+        load_words(tab2_win[0], tab2_words, 0, whole)
+        load_scale_rows(tab2_plane, tab2_scales, range(4))
+        w2_raw[1, 0] = load_weight(w2, 1, 0, "w2_raw10")
+        load_words(tab2_win[1], tab2_words, 1, low)
+        load_words(tab2_win[1], tab2_words, 1, high)
+        idx1 = load_list(offs, "idx1")
+        load_scale_rows(tab1_plane, tab_scales, range(4))
+        p2 = load_list(pos2, "p2")
+        p3 = load_list(pos3, "p3")
+        w1_raw = {0: load_weight(w1, 0, 0, "w1_raw0")}
+        p1 = load_list(pos1, "p1")
+        gains = keep.tile([P, 2, PACK], F32, name="gains")
+        nc.sync.dma_start(gains[:], gain.rearrange("(g p t) -> p g t", g=2, t=PACK))
+        tab1_win = table_tile("tab1_win")
+        load_words(tab1_win, tab_words, 0, whole)
+        for a in range(2):
+            w2_raw[a, 1] = load_weight(w2, a, 1, "w2_raw%d1" % a)
+        w1_raw[1] = load_weight(w1, 0, 1, "w1_raw1")
+        w4_raw = [load_weight(w4, g, 0, "w4_raw%d" % g) for g in range(2)]
+
+        w3_codes = keep.tile([P, 2 * H], U8, name="w3_codes", align_bytes=64)
+        nc.vector.tensor_copy(
+            w3_codes[:].rearrange("p (g t m b) -> p g m t b", g=2, t=PACK, b=2),
+            w3_raw[:].rearrange("p (g m t b) -> p g m t b", g=2, t=PACK, b=2),
+        )
+        w3_plane = keep.tile([P, H], U8, name="w3_plane", align_bytes=64)
+        nc.vector.tensor_copy(
+            w3_plane[:].rearrange("p (g t m) -> p g m t", g=2, t=PACK),
+            w3_plane_raw[:].rearrange("p (g m t) -> p g m t", g=2, t=PACK),
+        )
+        v3_words = gather_words(tab3_win, idx3, "v3_words", 1)
+        v3_scales = gather_scales(tab3_plane, idx3, "v3_scales")
+        w2_q = {(0, 0): quantize_weight(w2_raw[0, 0], "w2_00", nc.vector.tensor_copy)}
+        v2_words = [gather_words(tab2_win[0], idx2, "v2_words0", 1)]
+        v2_scales = gather_scales(tab2_plane, idx2, "v2_scales")
+        w2_q[1, 0] = quantize_weight(w2_raw[1, 0], "w2_10", nc.vector.tensor_copy)
+        v2_words.append(gather_words(tab2_win[1], idx2, "v2_words1", 2))
+        v1_scales = gather_scales(tab1_plane, idx1, "v1_scales")
+        v2 = [(v2_words[a], v2_scales, 4 * a) for a in range(2)]
+        w1_q, w4_q, z_q, v1 = {}, {}, {}, []
+        d_rows, b_rows, a_rows, bill, bounded, z = {}, {}, {}, {}, {}, {}
+
+        def make_d(k):
+            lhs = (w3_codes[:, 2 * P * k : 2 * P * (k + 1)].bitcast(E2M1), w3_plane[:, P * k : P * (k + 1)])
+            d_rows[k] = first_stage([lhs], [(v3_words, v3_scales, 0)], "d_rows", "d_rows", 8)
+
+        def make_b(k):
+            g, t = divmod(k, PACK)
+            b_rows[k] = first_stage([slot(w2_q[a, g], t) for a in range(2)], v2, "b_rows", "rows", 6)
+
+        def make_a(k):
+            g, t = divmod(k, PACK)
+            a_rows[k] = first_stage([slot(w1_q[g], t)], v1, "a_rows", "rows", 6)
+
+        def gathered_product(rows, offsets, other):
+            dst = ring.tile([P, VOTES], F32, name="product", tag="product", bufs=4)
+            nc.vector.tensor_tensor(dst[:], rows[:].indirect(offsets[:]), other[:], MULT)
+            return dst
+
+        def bound(product, k, side):
+            g, t = divmod(k, PACK)
+            if g not in bounded:
+                bounded[g] = ring.tile([P, 2, PACK, VOTES], F32, name="bounded", tag="big", bufs=3, align_bytes=64)
+            turned = next_bank()
+            for c in range(CHUNKS):
+                nc.tensor.transpose(turned[:, P * c : P * (c + 1)], product[:, CHUNK * c : CHUNK * (c + 1)], identity[:])
+            nc.scalar.activation(
+                bounded[g][:, side, t, :], turned[:], TANH, scale=(1.0, -1.0)[side]
+            )
+
+        def pick_bill(k):
+            bill[k] = ring.tile([P, VOTES], F32, name="bill", tag="bill", bufs=5)
+            nc.vector.tensor_copy(bill[k][:], b_rows[k][:].indirect(p2[:]))
+
+        def weigh(g, c):
+            if c == 0:
+                z[g] = ring.tile([P, PACK * VOTES], BF16, name="z", tag="z", bufs=1, align_bytes=64)
+                z_codes = keep.tile([P, VOTES], U32, name="z_codes%d" % g, align_bytes=64)
+                z_scales = keep.tile([P, VOTES], U8, name="z_scales%d" % g, align_bytes=64)
+                z_q[g] = (z_codes, z_scales)
+            diff = next_bank()
+            for t in range(PACK):
+                for side in range(2):
+                    nc.tensor.matmul(
+                        diff[:, CHUNK * t : CHUNK * (t + 1)], lhsT=bounded[g][:, side, t, P * c : P * (c + 1)], rhs=identity[:],
+                        is_transpose=True, start=(side == 0), stop=(side == 1),
+                    )
+            nc.vector.tensor_tensor(
+                z[g][:, BANK * c : BANK * (c + 1)].rearrange("p (j t) -> p j t", t=PACK),
+                diff[:].rearrange("p (t j) -> p j t", t=PACK),
+                gains[:, g, :].unsqueeze(1).broadcast_to([P, CHUNK, PACK]),
+                MULT,
+            )
+
+        def quantize_z(g, first, count):
+            cols = slice(CHUNK * first, CHUNK * (first + count))
+            wide = slice(BANK * first, BANK * (first + count))
+            nc.vector.quantize_mx(z_q[g][0][:, cols].bitcast(E4M3), z_q[g][1][:, cols], z[g][:, wide])
+
+        steps = 4 * PACK
+        AHEAD = 3
+        BEHIND = 2
+        product = {}
+
+        def which(i):
+            g, rest = divmod(i, 2 * PACK)
+            side, t = divmod(rest, PACK)
+            return PACK * g + t, 1 - side
+
+        def make_rows(i):
+            k, side = which(i)
+            (make_a, make_b)[side](k)
+
+        def meet(i):
+            k, side = which(i)
+            if side == 1:
+                pick_bill(k)
+                product[i] = gathered_product(d_rows[k], p3, bill[k])
+            else:
+                product[i] = gathered_product(a_rows[k], p1, bill[k])
+
+        for k in range(2 * PACK):
+            make_d(k)
+        for i in range(-AHEAD, steps + BEHIND):
+            if i == -1:
+                w1_q[0] = quantize_weight(w1_raw[0], "w1_0", nc.scalar.copy)
+            if i == 1:
+                v1.append((gather_words(tab1_win, idx1, "v1_words", 2), v1_scales, 0))
+            if i == 1:
+                w2_q[0, 1] = quantize_weight(w2_raw[0, 1], "w2_01", nc.scalar.copy)
+            if i == 2:
+                w2_q[1, 1] = quantize_weight(w2_raw[1, 1], "w2_11", nc.scalar.copy)
+            if i == 6:
+                w1_q[1] = quantize_weight(w1_raw[1], "w1_1", nc.scalar.copy)
+            if i == 9:
+                w4_q[0] = quantize_weight(w4_raw[0], "w4_0", nc.scalar.copy)
+            if i == 13:
+                w4_q[1] = quantize_weight(w4_raw[1], "w4_1", nc.scalar.copy)
+            if i + AHEAD < steps:
+                make_rows(i + AHEAD)
+            if 0 <= i < steps:
+                meet(i)
+            if i >= BEHIND:
+                bound(product[i - BEHIND], *which(i - BEHIND))
+            if 11 <= i < 11 + 2:
+                for c in range(2):
+                    weigh(0, 2 * (i - 11) + c)
+            if i == 11 + 2:
+                quantize_z(0, 0, CHUNKS)
+
+        y = ring.tile([P, PACK, VOTES], F32, name="y", tag="big", bufs=3, align_bytes=64)
+        y_bf = ring.tile([P, PACK * VOTES], BF16, name="y_bf", tag="grouped", bufs=2, align_bytes=64)
+        y_codes = keep.tile([P, VOTES], U32, name="y_codes", align_bytes=64)
+        y_scales = keep.tile([P, VOTES], U8, name="y_scales", align_bytes=64)
+        y_out = out_0.rearrange("(p t) j -> p t j", t=PACK)
+        words_out = out_1[0].rearrange("p m t -> p (m t)").bitcast(I32)
+
+        def last_product(c):
+            cols = slice(CHUNK * c, CHUNK * (c + 1))
+            acc = next_bank()
+            for t in range(PACK):
+                for g in range(2):
+                    lhs, lhs_scale = slot(w4_q[g], t)
+                    nc.tensor.matmul_mx(
+                        acc[:, CHUNK * t : CHUNK * (t + 1)], lhsT=lhs, lhsT_scale=lhs_scale,
+                        rhs=z_q[g][0][:, cols].bitcast(E4M3), rhs_scale=z_q[g][1][:, cols],
+                        start=(g == 0), stop=(g == 1),
+                    )
+            nc.scalar.copy(
+                y_bf[:, BANK * c : BANK * (c + 1)].rearrange("p (j t) -> p j t", t=PACK),
+                acc[:].rearrange("p (t j) -> p j t", t=PACK),
+            )
+            nc.scalar.copy(y[:, :, cols], acc[:].rearrange("p (t j) -> p t j", t=PACK))
+            nc.sync.dma_start(y_out[:, :, cols], y[:, :, cols])
+
+        def quantize_y(c):
+            cols = slice(CHUNK * c, CHUNK * (c + 1))
+            nc.vector.quantize_mx(y_codes[:, cols].bitcast(E4M3), y_scales[:, cols], y_bf[:, BANK * c : BANK * (c + 1)])
+            if c % 2 == 1:
+                pair = slice(CHUNK * (c - 1), CHUNK * (c + 1))
+                nc.sync.dma_start(words_out[:, pair], y_codes[:, pair].bitcast(I32))
+
+        for c in range(CHUNKS + 3):
+            if c < CHUNKS:
+                weigh(1, c)
+            if 1 <= c <= CHUNKS:
+                quantize_z(1, c - 1, 1)
+                last_product(c - 1)
+            if c >= 3:
+                quantize_y(c - 3)
+        for q in range(4):
+            nc.sync.dma_start(
+                out_2[0, 4 * q : 4 * q + 4, :].bitcast(I32),
+                y_scales[32 * q : 32 * q + 4, :].bitcast(I32),
+            )

@@ -1,7 +1,6 @@
 from contextlib import ExitStack
 
 import concourse.mybir as mybir
-from concourse.masks import make_identity
 
 F32 = mybir.dt.float32
 BF16 = mybir.dt.bfloat16
@@ -25,7 +24,8 @@ H = 1024
 N = 512
 BANK = 512
 HALF = VOTES // 2
-RAWB = 3
+RAWB = 5
+ROWB = 8
 CHUNK = 128
 CHUNKS = VOTES // CHUNK
 
@@ -57,18 +57,17 @@ def tile_list_roll_call_features_kernel(
             return dst
 
         def cleared_plane(width, name, engines):
-            dst = keep.tile([P, width], U8, name=name, align_bytes=64)
+            dst = keep.tile([P, width], U8, name=name, tag=name, align_bytes=64)
             share = width // len(engines)
             for e, engine in enumerate(engines):
                 engine.memset(dst[:, share * e : share * (e + 1)].bitcast(I32), 0)
             return dst
 
-        def load_scale_rows(dst, src, quadrants):
-            passes = src.shape[0]
-            for q in quadrants:
+        def load_scale_rows(dst, src, k):
+            rows = 4 * src.shape[0]
+            for q in range(4):
                 nc.sync.dma_start(
-                    dst[32 * q : 32 * q + 4 * passes, :].bitcast(I32),
-                    src[:, 4 * q : 4 * q + 4, :].bitcast(I32),
+                    dst[32 * q + k : 32 * q + k + rows, :].bitcast(I32), src[:, 4 * q : 4 * q + 4, :].bitcast(I32)
                 )
 
         def table_tile(name):
@@ -96,11 +95,12 @@ def tile_list_roll_call_features_kernel(
             nc.sync.dma_start(raw[:], rows.rearrange("(p j) c -> p j c", j=PACK))
             return raw
 
-        def quantize_weight(raw, name, cast):
+        def quantize_weight(raw, name, cast, run):
+            walk = "p q t j e" if run > 1 else "p q j t e"
             grouped = ring.tile([P, PACK * PASS], BF16, name=name + "_bf", tag="grouped", bufs=2, align_bytes=64)
             cast(
-                grouped[:].rearrange("p (t m j) -> p m j t", t=PACK, j=PACK),
-                raw[:].rearrange("p j (m t) -> p m j t", t=PACK),
+                grouped[:].rearrange("p (t q e j) -> " + walk, t=PACK, e=run, j=PACK),
+                raw[:].rearrange("p j (q t e) -> " + walk, t=PACK, e=run),
             )
             codes = keep.tile([P, PASS], U32, name=name + "_codes", align_bytes=64)
             scales = keep.tile([P, PASS], U8, name=name + "_scales", align_bytes=64)
@@ -126,76 +126,83 @@ def tile_list_roll_call_features_kernel(
             return codes[:, P * t : P * (t + 1)].bitcast(E4M3), scales[:, P * t : P * (t + 1)]
 
         whole, low, high = slice(0, T), slice(0, T // 2), slice(T // 2, T)
+        tab2_plane = cleared_plane(T, "tab2_plane", [nc.gpsimd, nc.vector])
         w3_plane_raw = cleared_plane(H, "w3_plane_raw", [nc.gpsimd])
-        tab3_plane = cleared_plane(T, "tab3_plane", [nc.gpsimd, nc.vector])
-        tab2_plane = cleared_plane(T, "tab2_plane", [nc.vector])
+        tab3_plane = cleared_plane(T, "tab3_plane", [nc.vector])
         tab1_plane = cleared_plane(T, "tab1_plane", [nc.vector])
-        identity = keep.tile([P, P], F32, name="identity")
-        make_identity(nc, identity[:])
-        w3_raw = keep.tile([P, 2 * H], U8, name="w3_raw")
-        nc.sync.dma_start(w3_raw[:].bitcast(I32), w3_words[0].bitcast(I32))
-        idx3 = load_list(offs3, "idx3")
-        idx2 = load_list(offs2, "idx2")
-        tab3_win = table_tile("tab3_win")
-        load_words(tab3_win, tab3_words, 0, low)
-        load_scale_rows(w3_plane_raw, w3_scales, range(4))
-        load_words(tab3_win, tab3_words, 0, high)
-        load_scale_rows(tab3_plane, tab3_scales, range(4))
-        w2_raw = {(0, 0): load_weight(w2, 0, 0, "w2_raw00")}
         tab2_win = [table_tile("tab2_win%d" % a) for a in range(2)]
-        load_words(tab2_win[0], tab2_words, 0, whole)
-        load_scale_rows(tab2_plane, tab2_scales, range(4))
+        idx2 = load_list(offs2, "idx2")
+        w2_raw = {(0, 0): load_weight(w2, 0, 0, "w2_raw00")}
+        load_words(tab2_win[0], tab2_words, 0, low)
+        load_words(tab2_win[0], tab2_words, 0, high)
+        load_scale_rows(tab2_plane, tab2_scales, 4)
+        idx3 = load_list(offs3, "idx3")
         w2_raw[1, 0] = load_weight(w2, 1, 0, "w2_raw10")
+        load_scale_rows(tab3_plane, tab3_scales, 0)
         load_words(tab2_win[1], tab2_words, 1, low)
         load_words(tab2_win[1], tab2_words, 1, high)
         idx1 = load_list(offs, "idx1")
-        load_scale_rows(tab1_plane, tab_scales, range(4))
+        load_scale_rows(tab1_plane, tab_scales, 12)
         p2 = load_list(pos2, "p2")
+        for a in range(2):
+            w2_raw[a, 1] = load_weight(w2, a, 1, "w2_raw%d1" % a)
+        w3_raw = keep.tile([P, 2 * H], U8, name="w3_raw")
+        nc.sync.dma_start(w3_raw[:].bitcast(I32), w3_words[0].bitcast(I32))
+        load_scale_rows(w3_plane_raw, w3_scales, 0)
+        tab3_win = table_tile("tab3_win")
+        load_words(tab3_win, tab3_words, 0, low)
+        load_words(tab3_win, tab3_words, 0, high)
         p3 = load_list(pos3, "p3")
         w1_raw = {0: load_weight(w1, 0, 0, "w1_raw0")}
         p1 = load_list(pos1, "p1")
-        gains = keep.tile([P, 2, PACK], F32, name="gains")
-        nc.sync.dma_start(gains[:], gain.rearrange("(g p t) -> p g t", g=2, t=PACK))
+        w1_raw[1] = load_weight(w1, 0, 1, "w1_raw1")
         tab1_win = table_tile("tab1_win")
         load_words(tab1_win, tab_words, 0, whole)
-        for a in range(2):
-            w2_raw[a, 1] = load_weight(w2, a, 1, "w2_raw%d1" % a)
-        w1_raw[1] = load_weight(w1, 0, 1, "w1_raw1")
-        w4_raw = [load_weight(w4, g, 0, "w4_raw%d" % g) for g in range(2)]
+        w4_raw = []
+        for g in range(2):
+            raw = ring.tile([P, PACK, PASS], F32, name="w4_raw", tag="raw", bufs=RAWB)
+            rows = w4.rearrange("(g q t e) n -> g t q e n", g=2, t=PACK, e=4)
+            for t in range(PACK):
+                nc.sync.dma_start(raw[:, t, :], rows[g, t])
+            w4_raw.append(raw)
+        gains = keep.tile([P, 2 * PACK, 8], F32, name="gains", tag="w3_plane_raw", align_bytes=64)
+        by_tile = gain.rearrange("(g q t e) -> g t q e", g=2, t=PACK, e=4)
+        with nc.allow_non_contiguous_dma(reason="one gain for each partition"):
+            for k in range(2 * PACK):
+                nc.sync.dma_start(gains[:, k, 0:1], by_tile[k // PACK, k % PACK])
 
-        w3_codes = keep.tile([P, 2 * H], U8, name="w3_codes", align_bytes=64)
-        nc.vector.tensor_copy(
-            w3_codes[:].rearrange("p (g t m b) -> p g m t b", g=2, t=PACK, b=2),
-            w3_raw[:].rearrange("p (g m t b) -> p g m t b", g=2, t=PACK, b=2),
-        )
-        w3_plane = keep.tile([P, H], U8, name="w3_plane", align_bytes=64)
-        nc.vector.tensor_copy(
-            w3_plane[:].rearrange("p (g t m) -> p g m t", g=2, t=PACK),
-            w3_plane_raw[:].rearrange("p (g m t) -> p g m t", g=2, t=PACK),
-        )
-        v3_words = gather_words(tab3_win, idx3, "v3_words", 1)
-        v3_scales = gather_scales(tab3_plane, idx3, "v3_scales")
-        w2_q = {(0, 0): quantize_weight(w2_raw[0, 0], "w2_00", nc.vector.tensor_copy)}
+        w2_q = {(0, 0): quantize_weight(w2_raw[0, 0], "w2_00", nc.scalar.copy, 4)}
         v2_words = [gather_words(tab2_win[0], idx2, "v2_words0", 1)]
         v2_scales = gather_scales(tab2_plane, idx2, "v2_scales")
-        w2_q[1, 0] = quantize_weight(w2_raw[1, 0], "w2_10", nc.vector.tensor_copy)
+        w2_q[1, 0] = quantize_weight(w2_raw[1, 0], "w2_10", nc.scalar.copy, 4)
+        v3_scales = gather_scales(tab3_plane, idx3, "v3_scales")
         v2_words.append(gather_words(tab2_win[1], idx2, "v2_words1", 2))
         v1_scales = gather_scales(tab1_plane, idx1, "v1_scales")
-        v2 = [(v2_words[a], v2_scales, 4 * a) for a in range(2)]
-        w1_q, w4_q, z_q, v1 = {}, {}, {}, []
+        v2 = [(v2_words[a], v2_scales, 4 + 4 * a) for a in range(2)]
+        w1_q, w4_q, z_q, v1, v3 = {}, {}, {}, [], []
         d_rows, b_rows, a_rows, bill, bounded, z = {}, {}, {}, {}, {}, {}
+        w3_codes = keep.tile([P, 2 * H], U8, name="w3_codes", align_bytes=64)
+        w3_plane = keep.tile([P, H], U8, name="w3_plane", align_bytes=64)
+
+        def deal_w3():
+            for dealt, raw, words in ((w3_codes, w3_raw, 2), (w3_plane, w3_plane_raw, 1)):
+                for g in range(2):
+                    nc.vector.tensor_copy(
+                        dealt[:].bitcast(I32).rearrange("p (g t q b) -> p g t q b", g=2, t=PACK, b=words)[:, g],
+                        raw[:].bitcast(I32).rearrange("p (g q t b) -> p g t q b", g=2, t=PACK, b=words)[:, g],
+                    )
 
         def make_d(k):
             lhs = (w3_codes[:, 2 * P * k : 2 * P * (k + 1)].bitcast(E2M1), w3_plane[:, P * k : P * (k + 1)])
-            d_rows[k] = first_stage([lhs], [(v3_words, v3_scales, 0)], "d_rows", "d_rows", 8)
+            d_rows[k] = first_stage([lhs], v3, "d_rows", "rows", ROWB)
 
         def make_b(k):
             g, t = divmod(k, PACK)
-            b_rows[k] = first_stage([slot(w2_q[a, g], t) for a in range(2)], v2, "b_rows", "rows", 6)
+            b_rows[k] = first_stage([slot(w2_q[a, g], t) for a in range(2)], v2, "b_rows", "rows", ROWB)
 
         def make_a(k):
             g, t = divmod(k, PACK)
-            a_rows[k] = first_stage([slot(w1_q[g], t)], v1, "a_rows", "rows", 6)
+            a_rows[k] = first_stage([slot(w1_q[g], t)], v1, "a_rows", "rows", ROWB)
 
         def gathered_product(rows, offsets, other):
             dst = ring.tile([P, VOTES], F32, name="product", tag="product", bufs=4)
@@ -206,15 +213,14 @@ def tile_list_roll_call_features_kernel(
             g, t = divmod(k, PACK)
             if g not in bounded:
                 bounded[g] = ring.tile([P, 2, PACK, VOTES], F32, name="bounded", tag="big", bufs=3, align_bytes=64)
-            turned = next_bank()
-            for c in range(CHUNKS):
-                nc.tensor.transpose(turned[:, P * c : P * (c + 1)], product[:, CHUNK * c : CHUNK * (c + 1)], identity[:])
-            nc.scalar.activation(
-                bounded[g][:, side, t, :], turned[:], TANH, scale=(1.0, -1.0)[side]
-            )
+            nc.scalar.activation(bounded[g][:, side, t, :], product[:], TANH)
+
+        def subtract(k):
+            g, t = divmod(k, PACK)
+            nc.vector.tensor_tensor(bounded[g][:, 0, t, :], bounded[g][:, 0, t, :], bounded[g][:, 1, t, :], SUB)
 
         def pick_bill(k):
-            bill[k] = ring.tile([P, VOTES], F32, name="bill", tag="bill", bufs=5)
+            bill[k] = ring.tile([P, VOTES], F32, name="bill", tag="bill", bufs=8)
             nc.vector.tensor_copy(bill[k][:], b_rows[k][:].indirect(p2[:]))
 
         def weigh(g, c):
@@ -223,17 +229,10 @@ def tile_list_roll_call_features_kernel(
                 z_codes = keep.tile([P, VOTES], U32, name="z_codes%d" % g, align_bytes=64)
                 z_scales = keep.tile([P, VOTES], U8, name="z_scales%d" % g, align_bytes=64)
                 z_q[g] = (z_codes, z_scales)
-            diff = next_bank()
-            for t in range(PACK):
-                for side in range(2):
-                    nc.tensor.matmul(
-                        diff[:, CHUNK * t : CHUNK * (t + 1)], lhsT=bounded[g][:, side, t, P * c : P * (c + 1)], rhs=identity[:],
-                        is_transpose=True, start=(side == 0), stop=(side == 1),
-                    )
             nc.vector.tensor_tensor(
-                z[g][:, BANK * c : BANK * (c + 1)].rearrange("p (j t) -> p j t", t=PACK),
-                diff[:].rearrange("p (t j) -> p j t", t=PACK),
-                gains[:, g, :].unsqueeze(1).broadcast_to([P, CHUNK, PACK]),
+                z[g][:, BANK * c : BANK * (c + 1)].rearrange("p (c i t) -> p c t i", i=4, t=PACK),
+                bounded[g][:, 0, :, CHUNK * c : CHUNK * (c + 1)].rearrange("p t (c i) -> p c t i", i=4),
+                gains[:, PACK * g : PACK * (g + 1), 0:1].unsqueeze(1).broadcast_to([P, CHUNK // 4, PACK, 4]),
                 MULT,
             )
 
@@ -242,55 +241,56 @@ def tile_list_roll_call_features_kernel(
             wide = slice(BANK * first, BANK * (first + count))
             nc.vector.quantize_mx(z_q[g][0][:, cols].bitcast(E4M3), z_q[g][1][:, cols], z[g][:, wide])
 
-        steps = 4 * PACK
+        tiles = 2 * PACK
+        steps = 3 * tiles
         AHEAD = 3
-        BEHIND = 2
+        BEHIND = 1
         product = {}
 
-        def which(i):
-            g, rest = divmod(i, 2 * PACK)
-            side, t = divmod(rest, PACK)
-            return PACK * g + t, 1 - side
-
         def make_rows(i):
-            k, side = which(i)
-            (make_a, make_b)[side](k)
+            stage, k = divmod(i, tiles)
+            (make_b, make_d, make_a)[stage](k)
 
         def meet(i):
-            k, side = which(i)
-            if side == 1:
+            stage, k = divmod(i, tiles)
+            if stage == 0:
                 pick_bill(k)
+            elif stage == 1:
                 product[i] = gathered_product(d_rows[k], p3, bill[k])
             else:
                 product[i] = gathered_product(a_rows[k], p1, bill[k])
 
-        for k in range(2 * PACK):
-            make_d(k)
         for i in range(-AHEAD, steps + BEHIND):
             if i == -1:
-                w1_q[0] = quantize_weight(w1_raw[0], "w1_0", nc.scalar.copy)
-            if i == 1:
-                v1.append((gather_words(tab1_win, idx1, "v1_words", 2), v1_scales, 0))
-            if i == 1:
-                w2_q[0, 1] = quantize_weight(w2_raw[0, 1], "w2_01", nc.scalar.copy)
-            if i == 2:
-                w2_q[1, 1] = quantize_weight(w2_raw[1, 1], "w2_11", nc.scalar.copy)
+                w2_q[0, 1] = quantize_weight(w2_raw[0, 1], "w2_01", nc.scalar.copy, 4)
+            if i == 0:
+                w2_q[1, 1] = quantize_weight(w2_raw[1, 1], "w2_11", nc.scalar.copy, 4)
+            if i == 4:
+                deal_w3()
+                v3.append((gather_words(tab3_win, idx3, "v3_words", 2), v3_scales, 0))
+            if i == 11:
+                v1.append((gather_words(tab1_win, idx1, "v1_words", 1), v1_scales, 12))
             if i == 6:
-                w1_q[1] = quantize_weight(w1_raw[1], "w1_1", nc.scalar.copy)
-            if i == 9:
-                w4_q[0] = quantize_weight(w4_raw[0], "w4_0", nc.scalar.copy)
-            if i == 13:
-                w4_q[1] = quantize_weight(w4_raw[1], "w4_1", nc.scalar.copy)
+                w1_q[0] = quantize_weight(w1_raw[0], "w1_0", nc.scalar.copy, 4)
+            if i == 12:
+                w1_q[1] = quantize_weight(w1_raw[1], "w1_1", nc.vector.tensor_copy, 4)
+            if i == 14:
+                w4_q[0] = quantize_weight(w4_raw[0], "w4_0", nc.vector.tensor_copy, 1)
+            if i == 22:
+                w4_q[1] = quantize_weight(w4_raw[1], "w4_1", nc.scalar.copy, 1)
             if i + AHEAD < steps:
                 make_rows(i + AHEAD)
             if 0 <= i < steps:
                 meet(i)
-            if i >= BEHIND:
-                bound(product[i - BEHIND], *which(i - BEHIND))
-            if 11 <= i < 11 + 2:
+            if i - BEHIND >= tiles:
+                stage, k = divmod(i - BEHIND, tiles)
+                bound(product[i - BEHIND], k, 2 - stage)
+                if stage == 2:
+                    subtract(k)
+            if 20 <= i < 20 + 2:
                 for c in range(2):
-                    weigh(0, 2 * (i - 11) + c)
-            if i == 11 + 2:
+                    weigh(0, 2 * (i - 20) + c)
+            if i == 20 + 2:
                 quantize_z(0, 0, CHUNKS)
 
         y = ring.tile([P, PACK, VOTES], F32, name="y", tag="big", bufs=3, align_bytes=64)
@@ -311,12 +311,14 @@ def tile_list_roll_call_features_kernel(
                         rhs=z_q[g][0][:, cols].bitcast(E4M3), rhs_scale=z_q[g][1][:, cols],
                         start=(g == 0), stop=(g == 1),
                     )
-            nc.scalar.copy(
+            (nc.scalar.copy if c < CHUNKS // 2 else nc.vector.tensor_copy)(
                 y_bf[:, BANK * c : BANK * (c + 1)].rearrange("p (j t) -> p j t", t=PACK),
                 acc[:].rearrange("p (t j) -> p j t", t=PACK),
             )
             nc.scalar.copy(y[:, :, cols], acc[:].rearrange("p (t j) -> p t j", t=PACK))
-            nc.sync.dma_start(y_out[:, :, cols], y[:, :, cols])
+            if c % 2 == 1:
+                done = slice(CHUNK * (c - 1), CHUNK * (c + 1))
+                nc.scalar.dma_start(y_out[:, :, done], y[:, :, done])
 
         def quantize_y(c):
             cols = slice(CHUNK * c, CHUNK * (c + 1))

@@ -12,24 +12,34 @@ E4M3 = mybir.dt.float8_e4m3fn_x4
 E2M1 = mybir.dt.float4_e2m1fn_x4
 MULT = mybir.AluOpType.mult
 SUB = mybir.AluOpType.subtract
+COPY = mybir.ActivationFunctionType.Copy
 TANH = mybir.ActivationFunctionType.Tanh
+
+K, K2, T, S, VOTES, H, N = 512, 1024, 4096, 1024, 512, 1024, 512
 
 P = 128
 PACK = 4
 PASS = P * PACK
-T = 4096
-S = 1024
-VOTES = 512
-H = 1024
-N = 512
+RUN = 4
+LINE = 4
+GROUPS = H // PASS
+TILES = GROUPS * PACK
 BANK = 512
-HALF = VOTES // 2
-RAWB = 5
-ROWB = 8
-CHUNK = 128
+BANKS = 8
+CHUNK = BANK // PACK
 CHUNKS = VOTES // CHUNK
+QUADRANTS = 4
+GAIN_PITCH = 8
 
-FLOPS = 2 * H * S * (512 + 1024 + 512) + 2 * H * N * VOTES
+SHIFT_V3, SHIFT_V2, SHIFT_V1 = 0, 4, 12
+
+AHEAD = 3
+RAW_BUFS = 4
+ROW_BUFS = 6
+BILL_AMENDMENT_BUFS = 3
+MEMBER_BILL_BUFS = 4
+
+FLOPS = 2 * H * S * (K + K2 + K) + 2 * H * N * VOTES
 
 
 def tile_list_roll_call_features_kernel(
@@ -44,37 +54,85 @@ def tile_list_roll_call_features_kernel(
         ring = ctx.enter_context(tc.tile_pool(name="ring", bufs=1))
         psum = ctx.enter_context(tc.psum_pool(name="psum", bufs=1))
 
-        banks = [psum.tile([P, BANK], F32, name="bank%d" % i) for i in range(8)]
-        used = []
+        banks = [psum.tile([P, BANK], F32, name="bank%d" % i) for i in range(BANKS)]
+        taken = []
 
         def next_bank():
-            used.append(banks[len(used) % len(banks)])
-            return used[-1]
+            taken.append(banks[len(taken) % BANKS])
+            return taken[-1]
+
 
         def load_list(src, name):
             dst = lists.tile(list(src.shape), U16, name=name)
             nc.sync.dma_start(dst[:], src)
             return dst
 
-        def cleared_plane(width, name, engines):
+        def cleared_plane(width, name, engine):
             dst = keep.tile([P, width], U8, name=name, tag=name, align_bytes=64)
-            share = width // len(engines)
-            for e, engine in enumerate(engines):
-                engine.memset(dst[:, share * e : share * (e + 1)].bitcast(I32), 0)
+            engine.memset(dst[:].bitcast(I32), 0)
             return dst
 
-        def load_scale_rows(dst, src, k):
+        def load_scale_rows(dst, src, shift, queue):
             rows = 4 * src.shape[0]
-            for q in range(4):
-                nc.sync.dma_start(
-                    dst[32 * q + k : 32 * q + k + rows, :].bitcast(I32), src[:, 4 * q : 4 * q + 4, :].bitcast(I32)
+            for quad in range(QUADRANTS):
+                first = 32 * quad + shift
+                queue.dma_start(
+                    dst[first : first + rows, :].bitcast(I32), src[:, 4 * quad : 4 * quad + 4, :].bitcast(I32)
                 )
 
-        def table_tile(name):
-            return ring.tile([P, T], I32, name=name, tag="big", bufs=3, align_bytes=64)
+        def load_table(words, a, name, tag, bufs, pieces):
+            dst = ring.tile([P, T], I32, name=name, tag=tag, bufs=bufs, align_bytes=64)
+            src = words[a].rearrange("p n t -> p (n t)").bitcast(I32)
+            for c in range(pieces):
+                cols = slice(T // pieces * c, T // pieces * (c + 1))
+                nc.sync.dma_start(dst[:, cols], src[:, cols])
+            return dst
 
-        def load_words(dst, words, a, cols):
-            nc.sync.dma_start(dst[:, cols], words[a].rearrange("p n t -> p (n t)").bitcast(I32)[:, cols])
+        def raw_tile():
+            return ring.tile([P, PACK, PASS], F32, name="raw", tag="raw", bufs=RAW_BUFS)
+
+        def load_weight(w, a, g):
+            raw = raw_tile()
+            rows = w[PASS * a : PASS * (a + 1), PASS * g : PASS * (g + 1)]
+            nc.sync.dma_start(raw[:], rows.rearrange("(p j) c -> p j c", j=PACK))
+            return raw
+
+        def load_w4(g):
+            raw = raw_tile()
+            rows = w4.rearrange("(g q t e) n -> g t q e n", g=GROUPS, t=PACK, e=RUN)
+            for t in range(PACK):
+                nc.sync.dma_start(raw[:, t, :], rows[g, t])
+            return raw
+
+        w3_plane_raw = cleared_plane(H, "w3_plane_raw", nc.gpsimd)
+        tab3_plane = cleared_plane(T, "tab3_plane", nc.vector)
+        tab2_plane = cleared_plane(T, "tab2_plane", nc.vector)
+        tab1_plane = cleared_plane(T, "tab1_plane", nc.vector)
+        load_scale_rows(tab3_plane, tab3_scales, SHIFT_V3, nc.gpsimd)
+        load_scale_rows(tab2_plane, tab2_scales, SHIFT_V2, nc.gpsimd)
+        load_scale_rows(tab1_plane, tab_scales, SHIFT_V1, nc.gpsimd)
+
+        idx3 = load_list(offs3, "idx3")
+        tab3_win = load_table(tab3_words, 0, "tab3_win", "wide", GROUPS, 2)
+        w3_raw = keep.tile([P, 2 * H], U8, name="w3_raw")
+        nc.sync.dma_start(w3_raw[:].bitcast(I32), w3_words[0].bitcast(I32))
+        load_scale_rows(w3_plane_raw, w3_scales, 0, nc.sync)
+        w2_raw = {(0, 0): load_weight(w2, 0, 0)}
+        p3 = load_list(pos3, "p3")
+        idx2 = load_list(offs2, "idx2")
+        tab2_win = [load_table(tab2_words, 0, "tab2_win0", "wide", GROUPS, 1)]
+        idx1 = load_list(offs, "idx1")
+        w2_raw[1, 0] = load_weight(w2, 1, 0)
+        w2_raw[0, 1] = load_weight(w2, 0, 1)
+        tab2_win.append(load_table(tab2_words, 1, "tab2_win1", "late", 1, 2))
+        p2 = load_list(pos2, "p2")
+        w2_raw[1, 1] = load_weight(w2, 1, 1)
+        p1 = load_list(pos1, "p1")
+        w1_raw = [load_weight(w1, 0, 0)]
+        tab1_win = load_table(tab_words, 0, "tab1_win", "last", 1, 1)
+        w1_raw.append(load_weight(w1, 0, 1))
+        w4_raw = [load_w4(g) for g in range(GROUPS)]
+
 
         def gather_words(window, offsets, name, pieces):
             dst = keep.tile([P, S], U32, name=name, align_bytes=64)
@@ -89,15 +147,8 @@ def tile_list_roll_call_features_kernel(
             nc.vector.tensor_copy(dst[:], window[:].indirect(offsets[:]))
             return dst
 
-        def load_weight(w, a, g, name):
-            raw = ring.tile([P, PACK, PASS], F32, name=name, tag="raw", bufs=RAWB)
-            rows = w[PASS * a : PASS * (a + 1), PASS * g : PASS * (g + 1)]
-            nc.sync.dma_start(raw[:], rows.rearrange("(p j) c -> p j c", j=PACK))
-            return raw
-
-        def quantize_weight(raw, name, cast, run):
-            walk = "p q t j e" if run > 1 else "p q j t e"
-            grouped = ring.tile([P, PACK * PASS], BF16, name=name + "_bf", tag="grouped", bufs=2, align_bytes=64)
+        def quantize_weight(raw, name, cast, run, walk):
+            grouped = ring.tile([P, PACK * PASS], BF16, name="grouped", tag="grouped", bufs=2, align_bytes=64)
             cast(
                 grouped[:].rearrange("p (t q e j) -> " + walk, t=PACK, e=run, j=PACK),
                 raw[:].rearrange("p j (q t e) -> " + walk, t=PACK, e=run),
@@ -107,236 +158,177 @@ def tile_list_roll_call_features_kernel(
             nc.vector.quantize_mx(codes[:].bitcast(E4M3), scales[:], grouped[:])
             return codes, scales
 
-        def first_stage(stationary, moving, name, tag, bufs):
-            rows = ring.tile([P, S], F32, name=name, tag=tag, bufs=bufs)
+        def quantize_row_weight(raw, name, cast):
+            return quantize_weight(raw, name, cast, RUN, "p q t j e")
+
+        def quantize_w4(g):
+            return quantize_weight(w4_raw[g], "w4_%d" % g, nc.scalar.copy, 1, "p q j t e")
+
+        def deal_w3(raw, name, words):
+            dealt = keep.tile(list(raw.shape), U8, name=name, align_bytes=64)
+            for g in range(GROUPS):
+                nc.vector.tensor_copy(
+                    dealt[:].bitcast(I32).rearrange("p (g t q b) -> p g t q b", g=GROUPS, t=PACK, b=words)[:, g],
+                    raw[:].bitcast(I32).rearrange("p (g q t b) -> p g t q b", g=GROUPS, t=PACK, b=words)[:, g],
+                )
+            return dealt
+
+        def output_tile(quantized, t):
+            codes, scales = quantized
+            return codes[:, P * t : P * (t + 1)].bitcast(E4M3), scales[:, P * t : P * (t + 1)]
+
+        def first_stage(stationary, moving):
+            rows = ring.tile([P, S], F32, name="rows", tag="rows", bufs=ROW_BUFS)
             for c in range(S // BANK):
                 cols = slice(BANK * c, BANK * (c + 1))
                 acc = next_bank()
-                for a, ((lhs, lhs_scale), (rhs, rhs_scale, k)) in enumerate(zip(stationary, moving)):
+                for a, ((lhs, lhs_scale), (words, plane, shift)) in enumerate(zip(stationary, moving)):
                     nc.tensor.matmul_mx(
                         acc[:], lhsT=lhs, lhsT_scale=lhs_scale,
-                        rhs=rhs[:, cols].bitcast(E4M3), rhs_scale=rhs_scale[k:P, cols],
+                        rhs=words[:, cols].bitcast(E4M3), rhs_scale=plane[shift:P, cols],
                         start=(a == 0), stop=(a == len(moving) - 1),
                     )
                 nc.scalar.copy(rows[:, cols], acc[:])
             return rows
 
-        def slot(quantized, t):
-            codes, scales = quantized
-            return codes[:, P * t : P * (t + 1)].bitcast(E4M3), scales[:, P * t : P * (t + 1)]
+        v3_scales = gather_scales(tab3_plane, idx3, "v3_scales")
+        w3_codes = deal_w3(w3_raw, "w3_codes", 2)
+        w3_plane = deal_w3(w3_plane_raw, "w3_plane", 1)
+        v3 = [(gather_words(tab3_win, idx3, "v3_words", 2), v3_scales, SHIFT_V3)]
+        w2_q = {(0, 0): quantize_row_weight(w2_raw[0, 0], "w2_00", nc.vector.tensor_copy)}
+        v2_scales = gather_scales(tab2_plane, idx2, "v2_scales")
+        v2_words = [gather_words(tab2_win[0], idx2, "v2_words0", 1)]
+        v1_scales = gather_scales(tab1_plane, idx1, "v1_scales")
+        w2_q[1, 0] = quantize_row_weight(w2_raw[1, 0], "w2_10", nc.scalar.copy)
+        v2_words.append(gather_words(tab2_win[1], idx2, "v2_words1", 2))
+        v2 = [(v2_words[a], v2_scales, SHIFT_V2 + 4 * a) for a in range(2)]
 
-        whole, low, high = slice(0, T), slice(0, T // 2), slice(T // 2, T)
-        tab2_plane = cleared_plane(T, "tab2_plane", [nc.gpsimd, nc.vector])
-        w3_plane_raw = cleared_plane(H, "w3_plane_raw", [nc.gpsimd])
-        tab3_plane = cleared_plane(T, "tab3_plane", [nc.vector])
-        tab1_plane = cleared_plane(T, "tab1_plane", [nc.vector])
-        tab2_win = [table_tile("tab2_win%d" % a) for a in range(2)]
-        idx2 = load_list(offs2, "idx2")
-        w2_raw = {(0, 0): load_weight(w2, 0, 0, "w2_raw00")}
-        load_words(tab2_win[0], tab2_words, 0, low)
-        load_words(tab2_win[0], tab2_words, 0, high)
-        load_scale_rows(tab2_plane, tab2_scales, 4)
-        idx3 = load_list(offs3, "idx3")
-        w2_raw[1, 0] = load_weight(w2, 1, 0, "w2_raw10")
-        load_scale_rows(tab3_plane, tab3_scales, 0)
-        load_words(tab2_win[1], tab2_words, 1, low)
-        load_words(tab2_win[1], tab2_words, 1, high)
-        idx1 = load_list(offs, "idx1")
-        load_scale_rows(tab1_plane, tab_scales, 12)
-        p2 = load_list(pos2, "p2")
-        for a in range(2):
-            w2_raw[a, 1] = load_weight(w2, a, 1, "w2_raw%d1" % a)
-        w3_raw = keep.tile([P, 2 * H], U8, name="w3_raw")
-        nc.sync.dma_start(w3_raw[:].bitcast(I32), w3_words[0].bitcast(I32))
-        load_scale_rows(w3_plane_raw, w3_scales, 0)
-        tab3_win = table_tile("tab3_win")
-        load_words(tab3_win, tab3_words, 0, low)
-        load_words(tab3_win, tab3_words, 0, high)
-        p3 = load_list(pos3, "p3")
-        w1_raw = {0: load_weight(w1, 0, 0, "w1_raw0")}
-        p1 = load_list(pos1, "p1")
-        w1_raw[1] = load_weight(w1, 0, 1, "w1_raw1")
-        tab1_win = table_tile("tab1_win")
-        load_words(tab1_win, tab_words, 0, whole)
-        w4_raw = []
-        for g in range(2):
-            raw = ring.tile([P, PACK, PASS], F32, name="w4_raw", tag="raw", bufs=RAWB)
-            rows = w4.rearrange("(g q t e) n -> g t q e n", g=2, t=PACK, e=4)
+        d_rows = []
+        for k in range(TILES):
+            lhs = (w3_codes[:, 2 * P * k : 2 * P * (k + 1)].bitcast(E2M1), w3_plane[:, P * k : P * (k + 1)])
+            d_rows.append(first_stage([lhs], v3))
+        amendment = []
+        for g, tag in enumerate(("early", "late")):
+            picked = ring.tile([P, PACK, VOTES], F32, name="amendment", tag=tag, bufs=1, align_bytes=64)
             for t in range(PACK):
-                nc.sync.dma_start(raw[:, t, :], rows[g, t])
-            w4_raw.append(raw)
-        gains = keep.tile([P, 2 * PACK, 8], F32, name="gains", tag="w3_plane_raw", align_bytes=64)
-        by_tile = gain.rearrange("(g q t e) -> g t q e", g=2, t=PACK, e=4)
+                nc.vector.tensor_copy(picked[:, t, :], d_rows[PACK * g + t][:].indirect(p3[:]))
+                amendment.append(picked[:, t, :])
+
+        gains = keep.tile([P, TILES, GAIN_PITCH], F32, name="gains", tag="w3_plane_raw", align_bytes=64)
+        by_tile = gain.rearrange("(g q t e) -> g t q e", g=GROUPS, t=PACK, e=RUN)
         with nc.allow_non_contiguous_dma(reason="one gain for each partition"):
-            for k in range(2 * PACK):
+            for k in range(TILES):
                 nc.sync.dma_start(gains[:, k, 0:1], by_tile[k // PACK, k % PACK])
 
-        w2_q = {(0, 0): quantize_weight(w2_raw[0, 0], "w2_00", nc.scalar.copy, 4)}
-        v2_words = [gather_words(tab2_win[0], idx2, "v2_words0", 1)]
-        v2_scales = gather_scales(tab2_plane, idx2, "v2_scales")
-        w2_q[1, 0] = quantize_weight(w2_raw[1, 0], "w2_10", nc.scalar.copy, 4)
-        v3_scales = gather_scales(tab3_plane, idx3, "v3_scales")
-        v2_words.append(gather_words(tab2_win[1], idx2, "v2_words1", 2))
-        v1_scales = gather_scales(tab1_plane, idx1, "v1_scales")
-        v2 = [(v2_words[a], v2_scales, 4 + 4 * a) for a in range(2)]
-        w1_q, w4_q, z_q, v1, v3 = {}, {}, {}, [], []
-        d_rows, b_rows, a_rows, bill, bounded, z = {}, {}, {}, {}, {}, {}
-        w3_codes = keep.tile([P, 2 * H], U8, name="w3_codes", align_bytes=64)
-        w3_plane = keep.tile([P, H], U8, name="w3_plane", align_bytes=64)
+        w1_q, w4_q, v1 = [], [], []
+        rows, bill, product, bounded, rounded, z, z_q = {}, {}, {}, {}, {}, {}, {}
 
-        def deal_w3():
-            for dealt, raw, words in ((w3_codes, w3_raw, 2), (w3_plane, w3_plane_raw, 1)):
-                for g in range(2):
-                    nc.vector.tensor_copy(
-                        dealt[:].bitcast(I32).rearrange("p (g t q b) -> p g t q b", g=2, t=PACK, b=words)[:, g],
-                        raw[:].bitcast(I32).rearrange("p (g q t b) -> p g t q b", g=2, t=PACK, b=words)[:, g],
-                    )
+        def make_rows(i):
+            g, t = divmod(i % TILES, PACK)
+            if i < TILES:
+                rows[i] = first_stage([output_tile(w2_q[a, g], t) for a in range(2)], v2)
+            else:
+                rows[i] = first_stage([output_tile(w1_q[g], t)], v1)
 
-        def make_d(k):
-            lhs = (w3_codes[:, 2 * P * k : 2 * P * (k + 1)].bitcast(E2M1), w3_plane[:, P * k : P * (k + 1)])
-            d_rows[k] = first_stage([lhs], v3, "d_rows", "rows", ROWB)
+        def multiply(i):
+            k = i % TILES
+            if i < TILES:
+                bill[k] = ring.tile([P, VOTES], F32, name="bill", tag="bill", bufs=TILES)
+                nc.vector.tensor_copy(bill[k][:], rows[i][:].indirect(p2[:]))
+                product[i] = ring.tile([P, VOTES], F32, name="bd", tag="bd", bufs=BILL_AMENDMENT_BUFS)
+                nc.vector.tensor_tensor(product[i][:], bill[k][:], amendment[k], MULT)
+            else:
+                product[i] = ring.tile([P, VOTES], F32, name="ab", tag="ab", bufs=MEMBER_BILL_BUFS)
+                nc.vector.tensor_tensor(product[i][:], rows[i][:].indirect(p1[:]), bill[k][:], MULT)
 
-        def make_b(k):
-            g, t = divmod(k, PACK)
-            b_rows[k] = first_stage([slot(w2_q[a, g], t) for a in range(2)], v2, "b_rows", "rows", ROWB)
-
-        def make_a(k):
-            g, t = divmod(k, PACK)
-            a_rows[k] = first_stage([slot(w1_q[g], t)], v1, "a_rows", "rows", ROWB)
-
-        def gathered_product(rows, offsets, other):
-            dst = ring.tile([P, VOTES], F32, name="product", tag="product", bufs=4)
-            nc.vector.tensor_tensor(dst[:], rows[:].indirect(offsets[:]), other[:], MULT)
-            return dst
-
-        def bound(product, k, side):
+        def bound(i):
+            k = i % TILES
             g, t = divmod(k, PACK)
             if g not in bounded:
-                bounded[g] = ring.tile([P, 2, PACK, VOTES], F32, name="bounded", tag="big", bufs=3, align_bytes=64)
-            nc.scalar.activation(bounded[g][:, side, t, :], product[:], TANH)
+                bounded[g] = ring.tile([P, 2, PACK, VOTES], F32, name="bounded", tag="wide", bufs=GROUPS, align_bytes=64)
+            nc.scalar.activation(bounded[g][:, i // TILES, t, :], product[i][:], TANH)
+            if i >= TILES:
+                nc.vector.tensor_tensor(bounded[g][:, 1, t, :], bounded[g][:, 1, t, :], bounded[g][:, 0, t, :], SUB)
+                if t == 0:
+                    rounded[g] = ring.tile([P, PACK, VOTES], BF16, name="rounded", tag="early", bufs=1, align_bytes=64)
+                nc.scalar.activation(rounded[g][:, t, :], bounded[g][:, 1, t, :], COPY, scale=gains[:, k, 0:1])
 
-        def subtract(k):
-            g, t = divmod(k, PACK)
-            nc.vector.tensor_tensor(bounded[g][:, 0, t, :], bounded[g][:, 0, t, :], bounded[g][:, 1, t, :], SUB)
+        def interleave(dst, src, c):
+            nc.vector.tensor_copy(
+                dst[:, BANK * c : BANK * (c + 1)].rearrange("p (x i t) -> p x t i", i=LINE, t=PACK),
+                src[:, :, CHUNK * c : CHUNK * (c + 1)].rearrange("p t (x i) -> p x t i", i=LINE),
+            )
 
-        def pick_bill(k):
-            bill[k] = ring.tile([P, VOTES], F32, name="bill", tag="bill", bufs=8)
-            nc.vector.tensor_copy(bill[k][:], b_rows[k][:].indirect(p2[:]))
-
-        def weigh(g, c):
+        def interleave_z(g, c):
             if c == 0:
                 z[g] = ring.tile([P, PACK * VOTES], BF16, name="z", tag="z", bufs=1, align_bytes=64)
                 z_codes = keep.tile([P, VOTES], U32, name="z_codes%d" % g, align_bytes=64)
                 z_scales = keep.tile([P, VOTES], U8, name="z_scales%d" % g, align_bytes=64)
                 z_q[g] = (z_codes, z_scales)
-            nc.vector.tensor_tensor(
-                z[g][:, BANK * c : BANK * (c + 1)].rearrange("p (c i t) -> p c t i", i=4, t=PACK),
-                bounded[g][:, 0, :, CHUNK * c : CHUNK * (c + 1)].rearrange("p t (c i) -> p c t i", i=4),
-                gains[:, PACK * g : PACK * (g + 1), 0:1].unsqueeze(1).broadcast_to([P, CHUNK // 4, PACK, 4]),
-                MULT,
-            )
+            interleave(z[g], rounded[g], c)
 
-        def quantize_z(g, first, count):
+        def quantize_chunks(codes, scales, src, first, count):
             cols = slice(CHUNK * first, CHUNK * (first + count))
-            wide = slice(BANK * first, BANK * (first + count))
-            nc.vector.quantize_mx(z_q[g][0][:, cols].bitcast(E4M3), z_q[g][1][:, cols], z[g][:, wide])
+            nc.vector.quantize_mx(codes[:, cols].bitcast(E4M3), scales[:, cols], src[:, BANK * first : BANK * (first + count)])
 
-        tiles = 2 * PACK
-        steps = 3 * tiles
-        AHEAD = 3
-        BEHIND = 1
-        product = {}
-
-        def make_rows(i):
-            stage, k = divmod(i, tiles)
-            (make_b, make_d, make_a)[stage](k)
-
-        def meet(i):
-            stage, k = divmod(i, tiles)
-            if stage == 0:
-                pick_bill(k)
-            elif stage == 1:
-                product[i] = gathered_product(d_rows[k], p3, bill[k])
-            else:
-                product[i] = gathered_product(a_rows[k], p1, bill[k])
-
-        for i in range(-AHEAD, steps + BEHIND):
-            if i == -1:
-                w2_q[0, 1] = quantize_weight(w2_raw[0, 1], "w2_01", nc.scalar.copy, 4)
-            if i == 0:
-                w2_q[1, 1] = quantize_weight(w2_raw[1, 1], "w2_11", nc.scalar.copy, 4)
-            if i == 4:
-                deal_w3()
-                v3.append((gather_words(tab3_win, idx3, "v3_words", 2), v3_scales, 0))
-            if i == 11:
-                v1.append((gather_words(tab1_win, idx1, "v1_words", 1), v1_scales, 12))
-            if i == 6:
-                w1_q[0] = quantize_weight(w1_raw[0], "w1_0", nc.scalar.copy, 4)
-            if i == 12:
-                w1_q[1] = quantize_weight(w1_raw[1], "w1_1", nc.vector.tensor_copy, 4)
-            if i == 14:
-                w4_q[0] = quantize_weight(w4_raw[0], "w4_0", nc.vector.tensor_copy, 1)
-            if i == 22:
-                w4_q[1] = quantize_weight(w4_raw[1], "w4_1", nc.scalar.copy, 1)
+        for a in range(2):
+            w2_q[a, 1] = quantize_row_weight(w2_raw[a, 1], "w2_%d1" % a, nc.scalar.copy)
+        steps = 2 * TILES
+        group_done = TILES + PACK
+        for i in range(-AHEAD, steps + 1):
+            if i > 0 and i % PACK == 1:
+                piece = i // PACK
+                if piece < GROUPS:
+                    w1_q.append(quantize_row_weight(w1_raw[piece], "w1_%d" % piece, nc.scalar.copy))
+                else:
+                    w4_q.append(quantize_w4(piece - GROUPS))
+                if piece == 0:
+                    v1.append((gather_words(tab1_win, idx1, "v1_words", 2), v1_scales, SHIFT_V1))
             if i + AHEAD < steps:
                 make_rows(i + AHEAD)
             if 0 <= i < steps:
-                meet(i)
-            if i - BEHIND >= tiles:
-                stage, k = divmod(i - BEHIND, tiles)
-                bound(product[i - BEHIND], k, 2 - stage)
-                if stage == 2:
-                    subtract(k)
-            if 20 <= i < 20 + 2:
-                for c in range(2):
-                    weigh(0, 2 * (i - 20) + c)
-            if i == 20 + 2:
-                quantize_z(0, 0, CHUNKS)
+                multiply(i)
+            if i >= 1:
+                bound(i - 1)
+            if i - group_done in (0, 1):
+                for c in range(CHUNKS // 2):
+                    interleave_z(0, CHUNKS // 2 * (i - group_done) + c)
+            if i - group_done == 2:
+                quantize_chunks(*z_q[0], z[0], 0, CHUNKS)
 
-        y = ring.tile([P, PACK, VOTES], F32, name="y", tag="big", bufs=3, align_bytes=64)
-        y_bf = ring.tile([P, PACK * VOTES], BF16, name="y_bf", tag="grouped", bufs=2, align_bytes=64)
+        y = ring.tile([P, PACK, VOTES], F32, name="y", tag="last", bufs=1, align_bytes=64)
+        y_rounded = ring.tile([P, PACK * VOTES], BF16, name="y_rounded", tag="grouped", bufs=2, align_bytes=64)
         y_codes = keep.tile([P, VOTES], U32, name="y_codes", align_bytes=64)
         y_scales = keep.tile([P, VOTES], U8, name="y_scales", align_bytes=64)
         y_out = out_0.rearrange("(p t) j -> p t j", t=PACK)
-        words_out = out_1[0].rearrange("p m t -> p (m t)").bitcast(I32)
 
         def last_product(c):
             cols = slice(CHUNK * c, CHUNK * (c + 1))
             acc = next_bank()
-            for t in range(PACK):
-                for g in range(2):
-                    lhs, lhs_scale = slot(w4_q[g], t)
+            for g in range(GROUPS):
+                for t in range(PACK):
+                    lhs, lhs_scale = output_tile(w4_q[g], t)
                     nc.tensor.matmul_mx(
                         acc[:, CHUNK * t : CHUNK * (t + 1)], lhsT=lhs, lhsT_scale=lhs_scale,
                         rhs=z_q[g][0][:, cols].bitcast(E4M3), rhs_scale=z_q[g][1][:, cols],
-                        start=(g == 0), stop=(g == 1),
+                        start=(g == 0 and t == 0), stop=(g == GROUPS - 1 and t == PACK - 1),
                     )
-            (nc.scalar.copy if c < CHUNKS // 2 else nc.vector.tensor_copy)(
-                y_bf[:, BANK * c : BANK * (c + 1)].rearrange("p (j t) -> p j t", t=PACK),
-                acc[:].rearrange("p (t j) -> p j t", t=PACK),
-            )
             nc.scalar.copy(y[:, :, cols], acc[:].rearrange("p (t j) -> p t j", t=PACK))
-            if c % 2 == 1:
-                done = slice(CHUNK * (c - 1), CHUNK * (c + 1))
-                nc.scalar.dma_start(y_out[:, :, done], y[:, :, done])
-
-        def quantize_y(c):
-            cols = slice(CHUNK * c, CHUNK * (c + 1))
-            nc.vector.quantize_mx(y_codes[:, cols].bitcast(E4M3), y_scales[:, cols], y_bf[:, BANK * c : BANK * (c + 1)])
-            if c % 2 == 1:
-                pair = slice(CHUNK * (c - 1), CHUNK * (c + 1))
-                nc.sync.dma_start(words_out[:, pair], y_codes[:, pair].bitcast(I32))
+            nc.scalar.dma_start(y_out[:, :, cols], y[:, :, cols])
 
         for c in range(CHUNKS + 3):
             if c < CHUNKS:
-                weigh(1, c)
-            if 1 <= c <= CHUNKS:
-                quantize_z(1, c - 1, 1)
+                interleave_z(1, c)
+            if 0 <= c - 1 < CHUNKS:
+                quantize_chunks(*z_q[1], z[1], c - 1, 1)
                 last_product(c - 1)
-            if c >= 3:
-                quantize_y(c - 3)
-        for q in range(4):
-            nc.sync.dma_start(
-                out_2[0, 4 * q : 4 * q + 4, :].bitcast(I32),
-                y_scales[32 * q : 32 * q + 4, :].bitcast(I32),
+            if 0 <= c - 2 < CHUNKS:
+                interleave(y_rounded, y, c - 2)
+            if 0 <= c - 3:
+                quantize_chunks(y_codes, y_scales, y_rounded, c - 3, 1)
+        nc.sync.dma_start(out_1[0].rearrange("p m t -> p (m t)").bitcast(I32), y_codes[:].bitcast(I32))
+        for quad in range(QUADRANTS):
+            (nc.sync, nc.scalar)[quad % 2].dma_start(
+                out_2[0, 4 * quad : 4 * quad + 4, :].bitcast(I32),
+                y_scales[32 * quad : 32 * quad + 4, :].bitcast(I32),
             )

from contextlib import ExitStack

import concourse.mybir as mybir

F32 = mybir.dt.float32
BF16 = mybir.dt.bfloat16
I32 = mybir.dt.int32
U32 = mybir.dt.uint32
U16 = mybir.dt.uint16
U8 = mybir.dt.uint8
E4M3 = mybir.dt.float8_e4m3fn_x4
E2M1 = mybir.dt.float4_e2m1fn_x4
MULT = mybir.AluOpType.mult
SUB = mybir.AluOpType.subtract
COPY = mybir.ActivationFunctionType.Copy
TANH = mybir.ActivationFunctionType.Tanh

K, K2, T, S, VOTES, H, N = 512, 1024, 4096, 1024, 512, 1024, 512

P = 128
PACK = 4
PASS = P * PACK
RUN = 4
LINE = 4
GROUPS = H // PASS
TILES = GROUPS * PACK
BANK = 512
BANKS = 8
CHUNK = BANK // PACK
CHUNKS = VOTES // CHUNK
QUADRANTS = 4
GAIN_PITCH = 8

SHIFT_V3, SHIFT_V2, SHIFT_V1 = 0, 4, 12

AHEAD = 3
RAW_BUFS = 4
ROW_BUFS = 6
BILL_AMENDMENT_BUFS = 3
MEMBER_BILL_BUFS = 4

FLOPS = 2 * H * S * (K + K2 + K) + 2 * H * N * VOTES


def tile_list_roll_call_features_kernel(
    tc, tab_words, tab_scales, tab2_words, tab2_scales, tab3_words, tab3_scales,
    offs, offs2, offs3, pos1, pos2, pos3, w1, w2, w3_words, w3_scales, gain, w4,
    out_0, out_1, out_2,
):
    nc = tc.nc
    with ExitStack() as ctx:
        lists = ctx.enter_context(tc.tile_pool(name="lists", bufs=1))
        keep = ctx.enter_context(tc.tile_pool(name="keep", bufs=1))
        ring = ctx.enter_context(tc.tile_pool(name="ring", bufs=1))
        psum = ctx.enter_context(tc.psum_pool(name="psum", bufs=1))

        banks = [psum.tile([P, BANK], F32, name="bank%d" % i) for i in range(BANKS)]
        taken = []

        def next_bank():
            taken.append(banks[len(taken) % BANKS])
            return taken[-1]


        def load_list(src, name):
            dst = lists.tile(list(src.shape), U16, name=name)
            nc.sync.dma_start(dst[:], src)
            return dst

        def cleared_plane(width, name, engine):
            dst = keep.tile([P, width], U8, name=name, tag=name, align_bytes=64)
            engine.memset(dst[:].bitcast(I32), 0)
            return dst

        def load_scale_rows(dst, src, shift, queue):
            rows = 4 * src.shape[0]
            for quad in range(QUADRANTS):
                first = 32 * quad + shift
                queue.dma_start(
                    dst[first : first + rows, :].bitcast(I32), src[:, 4 * quad : 4 * quad + 4, :].bitcast(I32)
                )

        def load_table(words, a, name, tag, bufs, pieces):
            dst = ring.tile([P, T], I32, name=name, tag=tag, bufs=bufs, align_bytes=64)
            src = words[a].rearrange("p n t -> p (n t)").bitcast(I32)
            for c in range(pieces):
                cols = slice(T // pieces * c, T // pieces * (c + 1))
                nc.sync.dma_start(dst[:, cols], src[:, cols])
            return dst

        def raw_tile():
            return ring.tile([P, PACK, PASS], F32, name="raw", tag="raw", bufs=RAW_BUFS)

        def load_weight(w, a, g):
            raw = raw_tile()
            rows = w[PASS * a : PASS * (a + 1), PASS * g : PASS * (g + 1)]
            nc.sync.dma_start(raw[:], rows.rearrange("(p j) c -> p j c", j=PACK))
            return raw

        def load_w4(g):
            raw = raw_tile()
            rows = w4.rearrange("(g q t e) n -> g t q e n", g=GROUPS, t=PACK, e=RUN)
            for t in range(PACK):
                nc.sync.dma_start(raw[:, t, :], rows[g, t])
            return raw

        w3_plane_raw = cleared_plane(H, "w3_plane_raw", nc.gpsimd)
        tab3_plane = cleared_plane(T, "tab3_plane", nc.vector)
        tab2_plane = cleared_plane(T, "tab2_plane", nc.vector)
        tab1_plane = cleared_plane(T, "tab1_plane", nc.vector)
        load_scale_rows(tab3_plane, tab3_scales, SHIFT_V3, nc.gpsimd)
        load_scale_rows(tab2_plane, tab2_scales, SHIFT_V2, nc.gpsimd)
        load_scale_rows(tab1_plane, tab_scales, SHIFT_V1, nc.gpsimd)

        idx3 = load_list(offs3, "idx3")
        tab3_win = load_table(tab3_words, 0, "tab3_win", "wide", GROUPS, 2)
        w3_raw = keep.tile([P, 2 * H], U8, name="w3_raw")
        nc.sync.dma_start(w3_raw[:].bitcast(I32), w3_words[0].bitcast(I32))
        load_scale_rows(w3_plane_raw, w3_scales, 0, nc.sync)
        w2_raw = {(0, 0): load_weight(w2, 0, 0)}
        p3 = load_list(pos3, "p3")
        idx2 = load_list(offs2, "idx2")
        tab2_win = [load_table(tab2_words, 0, "tab2_win0", "wide", GROUPS, 1)]
        idx1 = load_list(offs, "idx1")
        w2_raw[1, 0] = load_weight(w2, 1, 0)
        w2_raw[0, 1] = load_weight(w2, 0, 1)
        tab2_win.append(load_table(tab2_words, 1, "tab2_win1", "late", 1, 2))
        p2 = load_list(pos2, "p2")
        w2_raw[1, 1] = load_weight(w2, 1, 1)
        p1 = load_list(pos1, "p1")
        w1_raw = [load_weight(w1, 0, 0)]
        tab1_win = load_table(tab_words, 0, "tab1_win", "last", 1, 1)
        w1_raw.append(load_weight(w1, 0, 1))
        w4_raw = [load_w4(g) for g in range(GROUPS)]


        def gather_words(window, offsets, name, pieces):
            dst = keep.tile([P, S], U32, name=name, align_bytes=64)
            n = S // pieces
            for c in range(pieces):
                part = offsets[:, n // 16 * c : n // 16 * (c + 1)]
                nc.vector.tensor_copy(dst[:, n * c : n * (c + 1)], window[:].bitcast(U32).indirect(part))
            return dst

        def gather_scales(window, offsets, name):
            dst = keep.tile([P, S], U8, name=name, align_bytes=64)
            nc.vector.tensor_copy(dst[:], window[:].indirect(offsets[:]))
            return dst

        def quantize_weight(raw, name, cast, run, walk):
            grouped = ring.tile([P, PACK * PASS], BF16, name="grouped", tag="grouped", bufs=2, align_bytes=64)
            cast(
                grouped[:].rearrange("p (t q e j) -> " + walk, t=PACK, e=run, j=PACK),
                raw[:].rearrange("p j (q t e) -> " + walk, t=PACK, e=run),
            )
            codes = keep.tile([P, PASS], U32, name=name + "_codes", align_bytes=64)
            scales = keep.tile([P, PASS], U8, name=name + "_scales", align_bytes=64)
            nc.vector.quantize_mx(codes[:].bitcast(E4M3), scales[:], grouped[:])
            return codes, scales

        def quantize_row_weight(raw, name, cast):
            return quantize_weight(raw, name, cast, RUN, "p q t j e")

        def quantize_w4(g):
            return quantize_weight(w4_raw[g], "w4_%d" % g, nc.scalar.copy, 1, "p q j t e")

        def deal_w3(raw, name, words):
            dealt = keep.tile(list(raw.shape), U8, name=name, align_bytes=64)
            for g in range(GROUPS):
                nc.vector.tensor_copy(
                    dealt[:].bitcast(I32).rearrange("p (g t q b) -> p g t q b", g=GROUPS, t=PACK, b=words)[:, g],
                    raw[:].bitcast(I32).rearrange("p (g q t b) -> p g t q b", g=GROUPS, t=PACK, b=words)[:, g],
                )
            return dealt

        def output_tile(quantized, t):
            codes, scales = quantized
            return codes[:, P * t : P * (t + 1)].bitcast(E4M3), scales[:, P * t : P * (t + 1)]

        def first_stage(stationary, moving):
            rows = ring.tile([P, S], F32, name="rows", tag="rows", bufs=ROW_BUFS)
            for c in range(S // BANK):
                cols = slice(BANK * c, BANK * (c + 1))
                acc = next_bank()
                for a, ((lhs, lhs_scale), (words, plane, shift)) in enumerate(zip(stationary, moving)):
                    nc.tensor.matmul_mx(
                        acc[:], lhsT=lhs, lhsT_scale=lhs_scale,
                        rhs=words[:, cols].bitcast(E4M3), rhs_scale=plane[shift:P, cols],
                        start=(a == 0), stop=(a == len(moving) - 1),
                    )
                nc.scalar.copy(rows[:, cols], acc[:])
            return rows

        v3_scales = gather_scales(tab3_plane, idx3, "v3_scales")
        w3_codes = deal_w3(w3_raw, "w3_codes", 2)
        w3_plane = deal_w3(w3_plane_raw, "w3_plane", 1)
        v3 = [(gather_words(tab3_win, idx3, "v3_words", 2), v3_scales, SHIFT_V3)]
        w2_q = {(0, 0): quantize_row_weight(w2_raw[0, 0], "w2_00", nc.vector.tensor_copy)}
        v2_scales = gather_scales(tab2_plane, idx2, "v2_scales")
        v2_words = [gather_words(tab2_win[0], idx2, "v2_words0", 1)]
        v1_scales = gather_scales(tab1_plane, idx1, "v1_scales")
        w2_q[1, 0] = quantize_row_weight(w2_raw[1, 0], "w2_10", nc.scalar.copy)
        v2_words.append(gather_words(tab2_win[1], idx2, "v2_words1", 2))
        v2 = [(v2_words[a], v2_scales, SHIFT_V2 + 4 * a) for a in range(2)]

        d_rows = []
        for k in range(TILES):
            lhs = (w3_codes[:, 2 * P * k : 2 * P * (k + 1)].bitcast(E2M1), w3_plane[:, P * k : P * (k + 1)])
            d_rows.append(first_stage([lhs], v3))
        amendment = []
        for g, tag in enumerate(("early", "late")):
            picked = ring.tile([P, PACK, VOTES], F32, name="amendment", tag=tag, bufs=1, align_bytes=64)
            for t in range(PACK):
                nc.vector.tensor_copy(picked[:, t, :], d_rows[PACK * g + t][:].indirect(p3[:]))
                amendment.append(picked[:, t, :])

        gains = keep.tile([P, TILES, GAIN_PITCH], F32, name="gains", tag="w3_plane_raw", align_bytes=64)
        by_tile = gain.rearrange("(g q t e) -> g t q e", g=GROUPS, t=PACK, e=RUN)
        with nc.allow_non_contiguous_dma(reason="one gain for each partition"):
            for k in range(TILES):
                nc.sync.dma_start(gains[:, k, 0:1], by_tile[k // PACK, k % PACK])

        w1_q, w4_q, v1 = [], [], []
        rows, bill, product, bounded, rounded, z, z_q = {}, {}, {}, {}, {}, {}, {}

        def make_rows(i):
            g, t = divmod(i % TILES, PACK)
            if i < TILES:
                rows[i] = first_stage([output_tile(w2_q[a, g], t) for a in range(2)], v2)
            else:
                rows[i] = first_stage([output_tile(w1_q[g], t)], v1)

        def multiply(i):
            k = i % TILES
            if i < TILES:
                bill[k] = ring.tile([P, VOTES], F32, name="bill", tag="bill", bufs=TILES)
                nc.vector.tensor_copy(bill[k][:], rows[i][:].indirect(p2[:]))
                product[i] = ring.tile([P, VOTES], F32, name="bd", tag="bd", bufs=BILL_AMENDMENT_BUFS)
                nc.vector.tensor_tensor(product[i][:], bill[k][:], amendment[k], MULT)
            else:
                product[i] = ring.tile([P, VOTES], F32, name="ab", tag="ab", bufs=MEMBER_BILL_BUFS)
                nc.vector.tensor_tensor(product[i][:], rows[i][:].indirect(p1[:]), bill[k][:], MULT)

        def bound(i):
            k = i % TILES
            g, t = divmod(k, PACK)
            if g not in bounded:
                bounded[g] = ring.tile([P, 2, PACK, VOTES], F32, name="bounded", tag="wide", bufs=GROUPS, align_bytes=64)
            nc.scalar.activation(bounded[g][:, i // TILES, t, :], product[i][:], TANH)
            if i >= TILES:
                nc.vector.tensor_tensor(bounded[g][:, 1, t, :], bounded[g][:, 1, t, :], bounded[g][:, 0, t, :], SUB)
                if t == 0:
                    rounded[g] = ring.tile([P, PACK, VOTES], BF16, name="rounded", tag="early", bufs=1, align_bytes=64)
                nc.scalar.activation(rounded[g][:, t, :], bounded[g][:, 1, t, :], COPY, scale=gains[:, k, 0:1])

        def interleave(dst, src, c):
            nc.vector.tensor_copy(
                dst[:, BANK * c : BANK * (c + 1)].rearrange("p (x i t) -> p x t i", i=LINE, t=PACK),
                src[:, :, CHUNK * c : CHUNK * (c + 1)].rearrange("p t (x i) -> p x t i", i=LINE),
            )

        def interleave_z(g, c):
            if c == 0:
                z[g] = ring.tile([P, PACK * VOTES], BF16, name="z", tag="z", bufs=1, align_bytes=64)
                z_codes = keep.tile([P, VOTES], U32, name="z_codes%d" % g, align_bytes=64)
                z_scales = keep.tile([P, VOTES], U8, name="z_scales%d" % g, align_bytes=64)
                z_q[g] = (z_codes, z_scales)
            interleave(z[g], rounded[g], c)

        def quantize_chunks(codes, scales, src, first, count):
            cols = slice(CHUNK * first, CHUNK * (first + count))
            nc.vector.quantize_mx(codes[:, cols].bitcast(E4M3), scales[:, cols], src[:, BANK * first : BANK * (first + count)])

        for a in range(2):
            w2_q[a, 1] = quantize_row_weight(w2_raw[a, 1], "w2_%d1" % a, nc.scalar.copy)
        steps = 2 * TILES
        group_done = TILES + PACK
        for i in range(-AHEAD, steps + 1):
            if i > 0 and i % PACK == 1:
                piece = i // PACK
                if piece < GROUPS:
                    w1_q.append(quantize_row_weight(w1_raw[piece], "w1_%d" % piece, nc.scalar.copy))
                else:
                    w4_q.append(quantize_w4(piece - GROUPS))
                if piece == 0:
                    v1.append((gather_words(tab1_win, idx1, "v1_words", 2), v1_scales, SHIFT_V1))
            if i + AHEAD < steps:
                make_rows(i + AHEAD)
            if 0 <= i < steps:
                multiply(i)
            if i >= 1:
                bound(i - 1)
            if i - group_done in (0, 1):
                for c in range(CHUNKS // 2):
                    interleave_z(0, CHUNKS // 2 * (i - group_done) + c)
            if i - group_done == 2:
                quantize_chunks(*z_q[0], z[0], 0, CHUNKS)

        y = ring.tile([P, PACK, VOTES], F32, name="y", tag="last", bufs=1, align_bytes=64)
        y_rounded = ring.tile([P, PACK * VOTES], BF16, name="y_rounded", tag="grouped", bufs=2, align_bytes=64)
        y_codes = keep.tile([P, VOTES], U32, name="y_codes", align_bytes=64)
        y_scales = keep.tile([P, VOTES], U8, name="y_scales", align_bytes=64)
        y_out = out_0.rearrange("(p t) j -> p t j", t=PACK)

        def last_product(c):
            cols = slice(CHUNK * c, CHUNK * (c + 1))
            acc = next_bank()
            for g in range(GROUPS):
                for t in range(PACK):
                    lhs, lhs_scale = output_tile(w4_q[g], t)
                    nc.tensor.matmul_mx(
                        acc[:, CHUNK * t : CHUNK * (t + 1)], lhsT=lhs, lhsT_scale=lhs_scale,
                        rhs=z_q[g][0][:, cols].bitcast(E4M3), rhs_scale=z_q[g][1][:, cols],
                        start=(g == 0 and t == 0), stop=(g == GROUPS - 1 and t == PACK - 1),
                    )
            nc.scalar.copy(y[:, :, cols], acc[:].rearrange("p (t j) -> p t j", t=PACK))
            nc.scalar.dma_start(y_out[:, :, cols], y[:, :, cols])

        for c in range(CHUNKS + 3):
            if c < CHUNKS:
                interleave_z(1, c)
            if 0 <= c - 1 < CHUNKS:
                quantize_chunks(*z_q[1], z[1], c - 1, 1)
                last_product(c - 1)
            if 0 <= c - 2 < CHUNKS:
                interleave(y_rounded, y, c - 2)
            if 0 <= c - 3:
                quantize_chunks(y_codes, y_scales, y_rounded, c - 3, 1)
        nc.sync.dma_start(out_1[0].rearrange("p m t -> p (m t)").bitcast(I32), y_codes[:].bitcast(I32))
        for quad in range(QUADRANTS):
            (nc.sync, nc.scalar)[quad % 2].dma_start(
                out_2[0, 4 * quad : 4 * quad + 4, :].bitcast(I32),
                y_scales[32 * quad : 32 * quad + 4, :].bitcast(I32),
            )
